import numpy as np
import ml_dtypes


def mxq(x, axis, fmt="e4m3"):
    dtype, down = {"e4m3": (ml_dtypes.float8_e4m3fn, 7), "e5m2": (ml_dtypes.float8_e5m2, 14)}[fmt]
    v = np.moveaxis(np.asarray(x, np.float32).astype(ml_dtypes.bfloat16).astype(np.float64), axis, -1)
    blocks = v.reshape(v.shape[:-1] + (-1, 32))
    amax = np.abs(blocks).max(-1, keepdims=True)
    byte = np.maximum(np.where(amax > 0, np.frexp(amax)[1] - 1 + 127, 0) - down, 1)
    scale = np.exp2(byte - 127.0)
    codes = (blocks / scale).astype(np.float32).astype(dtype).astype(np.float64)
    return np.moveaxis((codes * scale).reshape(v.shape), -1, axis)


WIDE = False


def mx_kscale(k):
    if not WIDE:
        return np.ones(k)
    levels = np.array([10, -10, 5, -5, 0])
    if k % 512:
        return np.exp2(np.random.permutation(np.resize(levels, k // 32))).repeat(32)
    a = np.empty((k // 512, 16))
    for p in range(k // 512):
        a[p, :8] = np.random.permutation(np.resize(levels, 8))
        for g in range(8):
            far = levels[np.abs(levels - a[p, g]) >= 10]
            a[p, g + 8] = far[np.random.randint(len(far))]
    return np.exp2(a.ravel()).repeat(32)


def f64(x):
    return np.asarray(x).astype(np.float64)


def striped(idx):
    return np.tile(idx.reshape(-1, 16).T, (8, 1)).astype(np.uint16)


def unstriped(offs):
    return offs[:16].T.reshape(-1).astype(np.int64)


def pack_weight(w):
    k, n = w.shape
    w = f64(np.asarray(w, np.float32).astype(ml_dtypes.bfloat16)).reshape(k // 32, 32, n)
    amax = np.abs(w).max(1)
    byte = np.clip(np.where(amax > 0, np.frexp(amax)[1] - 1 + 127 - 7, 1), 1, 254)
    scaled = (w * np.exp2(127.0 - byte)[:, None, :]).reshape(k, n).astype(np.float32)
    words = np.ascontiguousarray(scaled.reshape(k // 512, 128, 4, n).transpose(0, 1, 3, 2)).astype(ml_dtypes.float8_e4m3fn).view(np.uint8)
    return words, np.ascontiguousarray(byte.astype(np.uint8).reshape(k // 512, 16, n))


def unpack_weight(words, scales):
    g, p, n, _ = words.shape
    vals = np.ascontiguousarray(words).view(ml_dtypes.float8_e4m3fn).astype(np.float64) * np.repeat(np.exp2(scales.astype(np.float64) - 127.0), 8, axis=1)[..., None]
    return vals.transpose(0, 1, 3, 2).reshape(g * 512, n)


K, T, S, N = 512, 1024, 256, 128
P = 2 ** 7


def setup_inputs():
    n = np.random.standard_normal
    s = mx_kscale(K)[:, None]
    packed_xT = pack_weight(n((K, T)) * s)
    return {
        "x_words": packed_xT[0],
        "x_scales": packed_xT[1],
        "w1": (n((K, N)) / np.sqrt(K) / s).astype(np.float32),
        "w2": (n((K, N)) / np.sqrt(K) / s).astype(np.float32),
        "w3": (n((K, N)) / np.sqrt(K) / s).astype(np.float32),
        "w4": (n((K, N)) / np.sqrt(K) / s).astype(np.float32),
        "gl": (np.tile(np.random.uniform(0.2, 1.6, T), (P, 1))).astype(np.float32),
        "gt": (np.tile(np.random.uniform(0.2, 1.6, T), (P, 1))).astype(np.float32),
        "gr": (np.tile(np.random.uniform(0.2, 1.6, T), (P, 1))).astype(np.float32),
        "gb": (np.tile(np.random.uniform(0.2, 1.6, T), (P, 1))).astype(np.float32),
        "offs": striped(np.random.permutation(T)[:S]),
    }


def reference(x_words, x_scales, w1, w2, w3, w4, gl, gt, gr, gb, offs):
    xq = unpack_weight(x_words, x_scales)[:, unstriped(offs)]
    yl = mxq(f64(w1), 0, "e4m3").T @ xq
    pl = np.log(np.exp(yl) + 1.0)
    yr = mxq(f64(w3), 0, "e4m3").T @ xq
    pr = np.log(np.exp(yr) + 1.0)
    yt = mxq(f64(w2), 0, "e4m3").T @ xq
    pt = np.log(np.exp(yt) + 1.0)
    yb = mxq(f64(w4), 0, "e4m3").T @ xq
    pb = np.log(np.exp(yb) + 1.0)
    isec = (np.minimum(pl, f64(gl)[:1][:, unstriped(offs)]) + np.minimum(pr, f64(gr)[:1][:, unstriped(offs)])) * (np.minimum(pt, f64(gt)[:1][:, unstriped(offs)]) + np.minimum(pb, f64(gb)[:1][:, unstriped(offs)]))
    uni = (pl + pr) * (pt + pb) + (f64(gl)[:1][:, unstriped(offs)] + f64(gr)[:1][:, unstriped(offs)]) * (f64(gt)[:1][:, unstriped(offs)] + f64(gb)[:1][:, unstriped(offs)]) - isec
    iou = isec / uni
    ew = np.maximum(pl, f64(gl)[:1][:, unstriped(offs)]) + np.maximum(pr, f64(gr)[:1][:, unstriped(offs)])
    eh = np.maximum(pt, f64(gt)[:1][:, unstriped(offs)]) + np.maximum(pb, f64(gb)[:1][:, unstriped(offs)])
    return -1.0 * iou + 1.0 + 0.25 * (((pr - pl - (f64(gr)[:1][:, unstriped(offs)]) + f64(gl)[:1][:, unstriped(offs)]) ** 2 + (pb - pt - (f64(gb)[:1][:, unstriped(offs)]) + f64(gt)[:1][:, unstriped(offs)]) ** 2) / ((ew) ** 2 + (eh) ** 2))

@@ -1,0 +1,228 @@
+from contextlib import ExitStack
+
+import concourse.mybir as mybir
+from concourse.masks import make_identity
+
+K, T, S, N = 512, 1024, 256, 128
+FLOPS = 2 * K * S * 4 * N
+
+F32 = mybir.dt.float32
+BF16 = mybir.dt.bfloat16
+I32 = mybir.dt.int32
+U32 = mybir.dt.uint32
+U16 = mybir.dt.uint16
+U8 = mybir.dt.uint8
+FP8X4 = mybir.dt.float8_e4m3fn_x4
+ACT = mybir.ActivationFunctionType
+ALU = mybir.AluOpType
+
+P = 128
+PACK = 4
+TILES = S // P
+SIDES = 4
+LINE = 4
+SCALAR_LINES = (32, 32, 0, 12)
+EXP_CAP = 2.0 ** 60
+
+
+def tile_picked_ygiou_diou_p_kernel(
+    tc, x_words, x_scales, w1, w2, w3, w4, gl, gt, gr, gb, offs, out
+):
+    nc = tc.nc
+    weights = (w1, w2, w3, w4)
+    truths = (gl, gt, gr, gb)
+
+    with ExitStack() as ctx:
+        keep = ctx.enter_context(tc.tile_pool(name="keep", bufs=1))
+        psum = ctx.enter_context(tc.psum_pool(name="psum", bufs=1))
+
+        offsets = keep.tile([P, S // 16], U16, name="offsets")
+        nc.sync.dma_start(offsets[:], offs)
+
+        word_window = keep.tile([P, T], U32, name="word_window", align_bytes=64)
+        nc.sync.dma_start(
+            word_window[:].bitcast(I32),
+            x_words[0].rearrange("p n t -> p (n t)").bitcast(I32),
+        )
+        scale_window = keep.tile([P, T], U8, name="scale_window", align_bytes=64)
+        nc.vector.memset(scale_window[:].bitcast(I32), 0)
+        for q in range(4):
+            nc.sync.dma_start(
+                scale_window[32 * q : 32 * q + 4, :].bitcast(I32),
+                x_scales[0][4 * q : 4 * q + 4, :].bitcast(I32),
+            )
+        raw = []
+        for s in range(SIDES):
+            tile = keep.tile([P, PACK, N], F32, name="raw%d" % s)
+            nc.sync.dma_start(tile[:], weights[s].rearrange("(p j) m -> p j m", j=PACK))
+            raw.append(tile)
+        truth_window = keep.tile([P, T], F32, name="truth_window", tag="wide")
+        zero = keep.tile([P, 1], F32, name="zero")
+        nc.vector.memset(zero[:], 0.0)
+        nc.scalar.copy(truth_window[:], zero[:].to_broadcast([P, T]))
+        for s in range(SIDES):
+            nc.sync.dma_start(truth_window[s : s + 1, :], truths[s][0:1, :])
+
+        identity = keep.tile([P, P], F32, name="identity")
+        make_identity(nc, identity[:])
+
+        x_codes = keep.tile([P, S], U32, name="x_codes", align_bytes=64)
+        x_bytes = keep.tile([P, S], U8, name="x_bytes", align_bytes=64)
+        nc.vector.tensor_copy(x_bytes[:], scale_window[:].indirect(offsets[:]))
+        nc.vector.tensor_copy(x_codes[:], word_window[:].indirect(offsets[:]))
+
+        grown = keep.tile([P, TILES, SIDES, N], F32, name="grown")
+        logits = []
+        for s in range(SIDES):
+            grouped = keep.tile([P, N, PACK], BF16, name="grouped%d" % s, align_bytes=64)
+            dst = grouped[:].rearrange("p (c i) j -> p c j i", i=LINE)
+            src = raw[s][:].rearrange("p j (c i) -> p c j i", i=LINE)
+            cut = SCALAR_LINES[s]
+            if cut > 0:
+                nc.scalar.copy(dst[:, :cut], src[:, :cut])
+            if cut < N // LINE:
+                nc.vector.tensor_copy(dst[:, cut:], src[:, cut:])
+            w_codes = keep.tile([P, N], U32, name="w_codes%d" % s, align_bytes=64)
+            w_bytes = keep.tile([P, N], U8, name="w_bytes%d" % s, align_bytes=64)
+            nc.vector.quantize_mx(
+                out=w_codes[:].bitcast(FP8X4),
+                scales=w_bytes[:],
+                in_=grouped[:].rearrange("p m j -> p (m j)"),
+            )
+            bank = psum.tile([P, TILES, N], F32, name="logits%d" % s)
+            for t in range(TILES):
+                cols = slice(t * P, (t + 1) * P)
+                nc.tensor.matmul_mx(
+                    out=bank[:, t, :],
+                    lhsT=x_codes[:, cols].bitcast(FP8X4),
+                    lhsT_scale=x_bytes[:, cols],
+                    rhs=w_codes[:].bitcast(FP8X4),
+                    rhs_scale=w_bytes[:],
+                    start=True,
+                    stop=True,
+                )
+            logits.append(bank)
+            nc.scalar.activation(grown[:, :, s, :], bank[:], ACT.Exp)
+
+        picked = keep.tile([P, S], F32, name="picked")
+        nc.vector.tensor_copy(picked[:], truth_window[:].indirect(offsets[:]))
+        capped = keep.tile([P, TILES, SIDES, N], F32, name="capped", tag="wide")
+        for t in range(TILES):
+            nc.vector.tensor_scalar(capped[:, t], grown[:, t], EXP_CAP, None, ALU.min)
+        turned = psum.tile([P, TILES, P], F32, name="turned", tag="spare")
+        for t in range(TILES):
+            nc.tensor.transpose(turned[:, t, :], picked[:, t * P : (t + 1) * P], identity[:])
+        truth = keep.tile([P, TILES, SIDES], F32, name="truth")
+        nc.vector.tensor_copy(truth[:], turned[:, :, 0:SIDES])
+        extent = keep.tile([P, TILES, 2], F32, name="extent")
+        shift = keep.tile([P, TILES, 2], F32, name="shift")
+        true_area = keep.tile([P, TILES], F32, name="true_area")
+        nc.vector.tensor_tensor(extent[:], truth[:, :, 0:2], truth[:, :, 2:4], ALU.add)
+        nc.vector.tensor_tensor(shift[:], truth[:, :, 0:2], truth[:, :, 2:4], ALU.subtract)
+        nc.vector.tensor_tensor(true_area[:], extent[:, :, 0], extent[:, :, 1], ALU.mult)
+
+        logs = keep.tile([P, TILES, SIDES, N], F32, name="logs")
+        for t in range(TILES):
+            for h in range(2):
+                nc.scalar.activation(logs[:, t, 2 * h : 2 * h + 2, :], capped[:, t, 2 * h : 2 * h + 2, :], ACT.Ln, bias=1.0)
+
+        def per_tile(name, slots):
+            return [keep.tile([P, slots, N], F32, name="%s%d" % (name, t)) for t in range(TILES)]
+
+        dist = per_tile("dist", SIDES)
+        near = per_tile("near", 2)
+        inner = per_tile("inner", 2)
+        size = per_tile("size", 2)
+        excess = per_tile("excess", 2)
+        skew = per_tile("skew", 2)
+        hull_sq = per_tile("hull_sq", 2)
+        skew_sq = per_tile("skew_sq", 2)
+        areas = per_tile("areas", 2)
+        root = per_tile("root", 2)
+        recip = per_tile("recip", 2)
+        ratio = per_tile("ratio", 2)
+        loss = per_tile("loss", 1)
+        overlap_bank = [psum.tile([P, 2, P], F32, name="overlap_bank%d" % t) for t in range(TILES)]
+        centre_bank = [
+            psum.tile([P, 2, P], F32, name="centre_bank%d" % t, tag="spare" if t else "centre") for t in range(TILES)
+        ]
+
+        def turn_and_add(dest, parts):
+            for i, part in enumerate(parts):
+                nc.tensor.matmul(
+                    dest, lhsT=part, rhs=identity[:], is_transpose=True, start=(i == 0), stop=(i == len(parts) - 1)
+                )
+
+        def softplus(t, sides):
+            for s in sides:
+                nc.vector.tensor_tensor(dist[t][:, s, :], logits[s][:, t, :], logs[:, t, s, :], ALU.max)
+
+        def spans(t):
+            for a in range(2):
+                nc.vector.tensor_scalar(near[t][:, a, :], dist[t][:, a, :], truth[:, t, a : a + 1], None, ALU.min)
+            nc.vector.tensor_tensor(size[t][:], dist[t][:, 0:2, :], dist[t][:, 2:4, :], ALU.add)
+            for a in range(2):
+                nc.vector.scalar_tensor_tensor(
+                    inner[t][:, a, :], dist[t][:, 2 + a, :], truth[:, t, 2 + a : 3 + a], near[t][:, a, :], ALU.min, ALU.add
+                )
+
+        def union(t):
+            nc.vector.tensor_tensor(areas[t][:, 0, :], size[t][:, 0, :], size[t][:, 1, :], ALU.mult)
+            nc.vector.scalar_tensor_tensor(
+                areas[t][:, 1, :], inner[t][:, 0, :], -1.0, inner[t][:, 1, :], ALU.mult, ALU.mult
+            )
+            turn_and_add(
+                overlap_bank[t][:, 0, :],
+                [true_area[:, t : t + 1].to_broadcast([P, P]), areas[t][:, 0, :], areas[t][:, 1, :]],
+            )
+            turn_and_add(overlap_bank[t][:, 1, :], [areas[t][:, 1, :]])
+
+        def hull(t):
+            nc.vector.tensor_tensor(excess[t][:], size[t][:], inner[t][:], ALU.subtract)
+            for a in range(2):
+                nc.scalar.activation(hull_sq[t][:, a, :], excess[t][:, a, :], ACT.Square, bias=extent[:, t, a : a + 1])
+            turn_and_add(centre_bank[t][:, 0, :], [hull_sq[t][:, a, :] for a in range(2)])
+
+        def centres(t):
+            nc.vector.tensor_tensor(skew[t][:], dist[t][:, 2:4, :], dist[t][:, 0:2, :], ALU.subtract)
+            for a in range(2):
+                nc.scalar.activation(skew_sq[t][:, a, :], skew[t][:, a, :], ACT.Square, bias=shift[:, t, a : a + 1])
+            turn_and_add(centre_bank[t][:, 1, :], [skew_sq[t][:, a, :] for a in range(2)])
+
+        def reciprocal(t, h, bank):
+            nc.scalar.activation(root[t][:, h, :], bank[:, 0, :], ACT.Abs_reciprocal_sqrt)
+            nc.scalar.activation(recip[t][:, h, :], root[t][:, h, :], ACT.Square)
+
+        def overlap_ratio(t):
+            nc.vector.tensor_tensor(ratio[t][:, 0, :], overlap_bank[t][:, 1, :], recip[t][:, 0, :], ALU.mult)
+
+        def centre_ratio(t):
+            nc.vector.scalar_tensor_tensor(
+                ratio[t][:, 1, :], centre_bank[t][:, 1, :], 0.25, recip[t][:, 1, :], ALU.mult, ALU.mult
+            )
+
+        def finish(t):
+            nc.vector.scalar_tensor_tensor(loss[t][:, 0, :], ratio[t][:, 1, :], 1.0, ratio[t][:, 0, :], ALU.add, ALU.add)
+            nc.sync.dma_start(out[:, t * P : (t + 1) * P], loss[t][:, 0, :])
+
+        softplus(0, range(SIDES))
+        spans(0)
+        softplus(1, (0, 1))
+        union(0)
+        reciprocal(0, 0, overlap_bank[0])
+        softplus(1, (2, 3))
+        hull(0)
+        centres(0)
+        reciprocal(0, 1, centre_bank[0])
+        spans(1)
+        centres(1)
+        hull(1)
+        union(1)
+        reciprocal(1, 1, centre_bank[1])
+        reciprocal(1, 0, overlap_bank[1])
+        overlap_ratio(0)
+        centre_ratio(0)
+        finish(0)
+        overlap_ratio(1)
+        centre_ratio(1)
+        finish(1)

@@ -126,6 +126,9 @@ def tile_picked_ygiou_diou_p_kernel(
             for h in range(2):
                 nc.scalar.activation(logs[:, t, 2 * h : 2 * h + 2, :], capped[:, t, 2 * h : 2 * h + 2, :], ACT.Ln, bias=1.0)
 
+        warm = keep.tile([P, 1], F32, name="warm")
+        nc.scalar.activation(warm[:], logs[:, TILES - 1, SIDES - 1, 0:1], ACT.Abs_reciprocal_sqrt)
+
         def per_tile(name, slots):
             return [keep.tile([P, slots, N], F32, name="%s%d" % (name, t)) for t in range(TILES)]
 

@@ -89,11 +89,16 @@ def tile_picked_ygiou_diou_p_kernel(
                 scales=w_bytes[:],
                 in_=grouped[:].rearrange("p m j -> p (m j)"),
             )
-            bank = psum.tile([P, TILES, N], F32, name="logits%d" % s)
+            if s < SIDES - 1:
+                bank = psum.tile([P, TILES, N], F32, name="logits%d" % s, tag="logits%d" % s)
+                parts = [bank[:, t, :] for t in range(TILES)]
+            else:
+                banks = [psum.tile([P, N], F32, name="last%d" % t, tag="last%d" % t) for t in range(TILES)]
+                parts = [banks[t][:] for t in range(TILES)]
             for t in range(TILES):
                 cols = slice(t * P, (t + 1) * P)
                 nc.tensor.matmul_mx(
-                    out=bank[:, t, :],
+                    out=parts[t],
                     lhsT=x_codes[:, cols].bitcast(FP8X4),
                     lhsT_scale=x_bytes[:, cols],
                     rhs=w_codes[:].bitcast(FP8X4),
@@ -101,8 +106,12 @@ def tile_picked_ygiou_diou_p_kernel(
                     start=True,
                     stop=True,
                 )
-            logits.append(bank)
-            nc.scalar.activation(grown[:, :, s, :], bank[:], ACT.Exp)
+            logits.append(parts)
+            if s < SIDES - 1:
+                nc.scalar.activation(grown[:, :, s, :], bank[:], ACT.Exp)
+            else:
+                for t in range(TILES):
+                    nc.scalar.activation(grown[:, t, s, :], parts[t], ACT.Exp)
 
         picked = keep.tile([P, S], F32, name="picked")
         nc.vector.tensor_copy(picked[:], truth_window[:].indirect(offsets[:]))
@@ -123,8 +132,9 @@ def tile_picked_ygiou_diou_p_kernel(
 
         logs = keep.tile([P, TILES, SIDES, N], F32, name="logs")
         for t in range(TILES):
-            for h in range(2):
-                nc.scalar.activation(logs[:, t, 2 * h : 2 * h + 2, :], capped[:, t, 2 * h : 2 * h + 2, :], ACT.Ln, bias=1.0)
+            step = 1 if t == 0 else 2
+            for s in range(0, SIDES, step):
+                nc.scalar.activation(logs[:, t, s : s + step, :], capped[:, t, s : s + step, :], ACT.Ln, bias=1.0)
 
         warm = keep.tile([P, 1], F32, name="warm")
         nc.scalar.activation(warm[:], logs[:, TILES - 1, SIDES - 1, 0:1], ACT.Abs_reciprocal_sqrt)
@@ -142,13 +152,14 @@ def tile_picked_ygiou_diou_p_kernel(
         skew_sq = per_tile("skew_sq", 2)
         areas = per_tile("areas", 2)
         root = per_tile("root", 2)
-        recip = per_tile("recip", 2)
+        half = per_tile("half", 2)
         ratio = per_tile("ratio", 2)
         loss = per_tile("loss", 1)
-        overlap_bank = [psum.tile([P, 2, P], F32, name="overlap_bank%d" % t) for t in range(TILES)]
-        centre_bank = [
-            psum.tile([P, 2, P], F32, name="centre_bank%d" % t, tag="spare" if t else "centre") for t in range(TILES)
+        union_bank = [psum.tile([P, P], F32, name="union_bank%d" % t) for t in range(TILES)]
+        hull_bank = [
+            psum.tile([P, P], F32, name="hull_bank%d" % t, tag="spare" if t else "last0") for t in range(TILES)
         ]
+        centre_bank = [psum.tile([P, 2, P], F32, name="centre_bank%d" % t, tag="logits%d" % t) for t in range(TILES)]
 
         def turn_and_add(dest, parts):
             for i, part in enumerate(parts):
@@ -158,12 +169,14 @@ def tile_picked_ygiou_diou_p_kernel(
 
         def softplus(t, sides):
             for s in sides:
-                nc.vector.tensor_tensor(dist[t][:, s, :], logits[s][:, t, :], logs[:, t, s, :], ALU.max)
+                nc.vector.tensor_tensor(dist[t][:, s, :], logits[s][t], logs[:, t, s, :], ALU.max)
 
-        def spans(t):
+        def sizes(t):
             for a in range(2):
                 nc.vector.tensor_scalar(near[t][:, a, :], dist[t][:, a, :], truth[:, t, a : a + 1], None, ALU.min)
             nc.vector.tensor_tensor(size[t][:], dist[t][:, 0:2, :], dist[t][:, 2:4, :], ALU.add)
+
+        def overlaps(t):
             for a in range(2):
                 nc.vector.scalar_tensor_tensor(
                     inner[t][:, a, :], dist[t][:, 2 + a, :], truth[:, t, 2 + a : 3 + a], near[t][:, a, :], ALU.min, ALU.add
@@ -174,58 +187,85 @@ def tile_picked_ygiou_diou_p_kernel(
             nc.vector.scalar_tensor_tensor(
                 areas[t][:, 1, :], inner[t][:, 0, :], -1.0, inner[t][:, 1, :], ALU.mult, ALU.mult
             )
+
+        def turn_union(t):
             turn_and_add(
-                overlap_bank[t][:, 0, :],
+                union_bank[t][:],
                 [true_area[:, t : t + 1].to_broadcast([P, P]), areas[t][:, 0, :], areas[t][:, 1, :]],
             )
-            turn_and_add(overlap_bank[t][:, 1, :], [areas[t][:, 1, :]])
+
+        def turn_overlap(t):
+            turn_and_add(centre_bank[t][:, 1, :], [areas[t][:, 1, :]])
 
         def hull(t):
             nc.vector.tensor_tensor(excess[t][:], size[t][:], inner[t][:], ALU.subtract)
             for a in range(2):
                 nc.scalar.activation(hull_sq[t][:, a, :], excess[t][:, a, :], ACT.Square, bias=extent[:, t, a : a + 1])
-            turn_and_add(centre_bank[t][:, 0, :], [hull_sq[t][:, a, :] for a in range(2)])
+
+        def turn_hull(t):
+            turn_and_add(hull_bank[t][:], [hull_sq[t][:, a, :] for a in range(2)])
 
         def centres(t):
             nc.vector.tensor_tensor(skew[t][:], dist[t][:, 2:4, :], dist[t][:, 0:2, :], ALU.subtract)
             for a in range(2):
                 nc.scalar.activation(skew_sq[t][:, a, :], skew[t][:, a, :], ACT.Square, bias=shift[:, t, a : a + 1])
-            turn_and_add(centre_bank[t][:, 1, :], [skew_sq[t][:, a, :] for a in range(2)])
 
-        def reciprocal(t, h, bank):
-            nc.scalar.activation(root[t][:, h, :], bank[:, 0, :], ACT.Abs_reciprocal_sqrt)
-            nc.scalar.activation(recip[t][:, h, :], root[t][:, h, :], ACT.Square)
+        def turn_centres(t):
+            turn_and_add(centre_bank[t][:, 0, :], [skew_sq[t][:, a, :] for a in range(2)])
+
+        def reciprocal(t, h, divisor):
+            nc.scalar.activation(root[t][:, h, :], divisor, ACT.Abs_reciprocal_sqrt)
+
+        def square_root(t):
+            nc.scalar.activation(half[t][:, 1, :], root[t][:, 1, :], ACT.Square)
 
         def overlap_ratio(t):
-            nc.vector.tensor_tensor(ratio[t][:, 0, :], overlap_bank[t][:, 1, :], recip[t][:, 0, :], ALU.mult)
+            nc.vector.tensor_tensor(half[t][:, 0, :], centre_bank[t][:, 1, :], root[t][:, 0, :], ALU.mult)
 
         def centre_ratio(t):
             nc.vector.scalar_tensor_tensor(
-                ratio[t][:, 1, :], centre_bank[t][:, 1, :], 0.25, recip[t][:, 1, :], ALU.mult, ALU.mult
+                ratio[t][:, 1, :], centre_bank[t][:, 0, :], 0.25, half[t][:, 1, :], ALU.mult, ALU.mult
             )
+
+        def second_root(t, h):
+            nc.vector.tensor_tensor(ratio[t][:, h, :], half[t][:, h, :], root[t][:, h, :], ALU.mult)
 
         def finish(t):
             nc.vector.scalar_tensor_tensor(loss[t][:, 0, :], ratio[t][:, 1, :], 1.0, ratio[t][:, 0, :], ALU.add, ALU.add)
             nc.sync.dma_start(out[:, t * P : (t + 1) * P], loss[t][:, 0, :])
 
         softplus(0, range(SIDES))
-        spans(0)
+        sizes(0)
         softplus(1, (0, 1))
-        union(0)
-        reciprocal(0, 0, overlap_bank[0])
+        overlaps(0)
         softplus(1, (2, 3))
         hull(0)
+        turn_hull(0)
+        sizes(1)
         centres(0)
-        reciprocal(0, 1, centre_bank[0])
-        spans(1)
-        centres(1)
+        turn_centres(0)
+        reciprocal(0, 1, hull_bank[0][:])
+        square_root(0)
+        overlaps(1)
+        union(0)
+        turn_union(0)
+        turn_overlap(0)
         hull(1)
+        reciprocal(0, 0, union_bank[0][:])
         union(1)
-        reciprocal(1, 1, centre_bank[1])
-        reciprocal(1, 0, overlap_bank[1])
-        overlap_ratio(0)
+        turn_union(1)
+        turn_hull(1)
+        turn_overlap(1)
+        centres(1)
+        turn_centres(1)
+        reciprocal(1, 0, union_bank[1][:])
+        reciprocal(1, 1, hull_bank[1][:])
+        square_root(1)
         centre_ratio(0)
-        finish(0)
+        overlap_ratio(0)
+        second_root(0, 0)
         overlap_ratio(1)
+        finish(0)
+        second_root(1, 0)
         centre_ratio(1)
         finish(1)

@@ -39,18 +39,23 @@ def tile_picked_ygiou_diou_p_kernel(
         offsets = keep.tile([P, S // 16], U16, name="offsets")
         nc.sync.dma_start(offsets[:], offs)
 
+        scale_window = keep.tile([P, T], U8, name="scale_window", align_bytes=64)
+        nc.vector.memset(scale_window[:].bitcast(I32), 0)
+
+        def load_scales(queue, q):
+            queue.dma_start(
+                scale_window[32 * q : 32 * q + 4, :].bitcast(I32),
+                x_scales[0][4 * q : 4 * q + 4, :].bitcast(I32),
+            )
+
+        load_scales(nc.scalar, 0)
         word_window = keep.tile([P, T], U32, name="word_window", align_bytes=64)
         nc.sync.dma_start(
             word_window[:].bitcast(I32),
             x_words[0].rearrange("p n t -> p (n t)").bitcast(I32),
         )
-        scale_window = keep.tile([P, T], U8, name="scale_window", align_bytes=64)
-        nc.vector.memset(scale_window[:].bitcast(I32), 0)
-        for q in range(4):
-            nc.sync.dma_start(
-                scale_window[32 * q : 32 * q + 4, :].bitcast(I32),
-                x_scales[0][4 * q : 4 * q + 4, :].bitcast(I32),
-            )
+        for q in range(1, 4):
+            load_scales(nc.sync, q)
         raw = []
         for s in range(SIDES):
             tile = keep.tile([P, PACK, N], F32, name="raw%d" % s)
@@ -206,7 +211,7 @@ def tile_picked_ygiou_diou_p_kernel(
             turn_and_add(hull_bank[t][:], [hull_sq[t][:, a, :] for a in range(2)])
 
         def centres(t):
-            nc.vector.tensor_tensor(skew[t][:], dist[t][:, 2:4, :], dist[t][:, 0:2, :], ALU.subtract)
+            (nc.vector if t else nc.gpsimd).tensor_tensor(skew[t][:], dist[t][:, 2:4, :], dist[t][:, 0:2, :], ALU.subtract)
             for a in range(2):
                 nc.scalar.activation(skew_sq[t][:, a, :], skew[t][:, a, :], ACT.Square, bias=shift[:, t, a : a + 1])
 
@@ -235,37 +240,36 @@ def tile_picked_ygiou_diou_p_kernel(
             nc.sync.dma_start(out[:, t * P : (t + 1) * P], loss[t][:, 0, :])
 
         softplus(0, range(SIDES))
-        sizes(0)
-        softplus(1, (0, 1))
-        overlaps(0)
-        softplus(1, (2, 3))
-        hull(0)
-        turn_hull(0)
-        sizes(1)
+        softplus(1, range(SIDES))
         centres(0)
-        turn_centres(0)
-        reciprocal(0, 1, hull_bank[0][:])
-        square_root(0)
+        sizes(0)
+        sizes(1)
+        overlaps(0)
         overlaps(1)
-        union(0)
-        turn_union(0)
-        turn_overlap(0)
+        hull(0)
         hull(1)
-        reciprocal(0, 0, union_bank[0][:])
-        union(1)
-        turn_union(1)
+        turn_centres(0)
+        turn_hull(0)
+        union(0)
         turn_hull(1)
-        turn_overlap(1)
-        centres(1)
-        turn_centres(1)
-        reciprocal(1, 0, union_bank[1][:])
+        reciprocal(0, 1, hull_bank[0][:])
+        union(1)
+        turn_union(0)
         reciprocal(1, 1, hull_bank[1][:])
+        centres(1)
+        turn_union(1)
+        square_root(0)
+        reciprocal(0, 0, union_bank[0][:])
+        turn_overlap(0)
+        turn_overlap(1)
+        reciprocal(1, 0, union_bank[1][:])
         square_root(1)
+        turn_centres(1)
         centre_ratio(0)
         overlap_ratio(0)
-        second_root(0, 0)
         overlap_ratio(1)
-        finish(0)
+        second_root(0, 0)
         second_root(1, 0)
         centre_ratio(1)
+        finish(0)
         finish(1)

from contextlib import ExitStack

import concourse.mybir as mybir
from concourse.masks import make_identity

K, T, S, N = 512, 1024, 256, 128
FLOPS = 2 * K * S * 4 * N

F32 = mybir.dt.float32
BF16 = mybir.dt.bfloat16
I32 = mybir.dt.int32
U32 = mybir.dt.uint32
U16 = mybir.dt.uint16
U8 = mybir.dt.uint8
FP8X4 = mybir.dt.float8_e4m3fn_x4
ACT = mybir.ActivationFunctionType
ALU = mybir.AluOpType

P = 128
PACK = 4
TILES = S // P
SIDES = 4
LINE = 4
SCALAR_LINES = (32, 32, 0, 12)
EXP_CAP = 2.0 ** 60


def tile_picked_ygiou_diou_p_kernel(
    tc, x_words, x_scales, w1, w2, w3, w4, gl, gt, gr, gb, offs, out
):
    nc = tc.nc
    weights = (w1, w2, w3, w4)
    truths = (gl, gt, gr, gb)

    with ExitStack() as ctx:
        keep = ctx.enter_context(tc.tile_pool(name="keep", bufs=1))
        psum = ctx.enter_context(tc.psum_pool(name="psum", bufs=1))

        offsets = keep.tile([P, S // 16], U16, name="offsets")
        nc.sync.dma_start(offsets[:], offs)

        scale_window = keep.tile([P, T], U8, name="scale_window", align_bytes=64)
        nc.vector.memset(scale_window[:].bitcast(I32), 0)

        def load_scales(queue, q):
            queue.dma_start(
                scale_window[32 * q : 32 * q + 4, :].bitcast(I32),
                x_scales[0][4 * q : 4 * q + 4, :].bitcast(I32),
            )

        load_scales(nc.scalar, 0)
        word_window = keep.tile([P, T], U32, name="word_window", align_bytes=64)
        nc.sync.dma_start(
            word_window[:].bitcast(I32),
            x_words[0].rearrange("p n t -> p (n t)").bitcast(I32),
        )
        for q in range(1, 4):
            load_scales(nc.sync, q)
        raw = []
        for s in range(SIDES):
            tile = keep.tile([P, PACK, N], F32, name="raw%d" % s)
            nc.sync.dma_start(tile[:], weights[s].rearrange("(p j) m -> p j m", j=PACK))
            raw.append(tile)
        truth_window = keep.tile([P, T], F32, name="truth_window", tag="wide")
        zero = keep.tile([P, 1], F32, name="zero")
        nc.vector.memset(zero[:], 0.0)
        nc.scalar.copy(truth_window[:], zero[:].to_broadcast([P, T]))
        for s in range(SIDES):
            nc.sync.dma_start(truth_window[s : s + 1, :], truths[s][0:1, :])

        identity = keep.tile([P, P], F32, name="identity")
        make_identity(nc, identity[:])

        x_codes = keep.tile([P, S], U32, name="x_codes", align_bytes=64)
        x_bytes = keep.tile([P, S], U8, name="x_bytes", align_bytes=64)
        nc.vector.tensor_copy(x_bytes[:], scale_window[:].indirect(offsets[:]))
        nc.vector.tensor_copy(x_codes[:], word_window[:].indirect(offsets[:]))

        grown = keep.tile([P, TILES, SIDES, N], F32, name="grown")
        logits = []
        for s in range(SIDES):
            grouped = keep.tile([P, N, PACK], BF16, name="grouped%d" % s, align_bytes=64)
            dst = grouped[:].rearrange("p (c i) j -> p c j i", i=LINE)
            src = raw[s][:].rearrange("p j (c i) -> p c j i", i=LINE)
            cut = SCALAR_LINES[s]
            if cut > 0:
                nc.scalar.copy(dst[:, :cut], src[:, :cut])
            if cut < N // LINE:
                nc.vector.tensor_copy(dst[:, cut:], src[:, cut:])
            w_codes = keep.tile([P, N], U32, name="w_codes%d" % s, align_bytes=64)
            w_bytes = keep.tile([P, N], U8, name="w_bytes%d" % s, align_bytes=64)
            nc.vector.quantize_mx(
                out=w_codes[:].bitcast(FP8X4),
                scales=w_bytes[:],
                in_=grouped[:].rearrange("p m j -> p (m j)"),
            )
            if s < SIDES - 1:
                bank = psum.tile([P, TILES, N], F32, name="logits%d" % s, tag="logits%d" % s)
                parts = [bank[:, t, :] for t in range(TILES)]
            else:
                banks = [psum.tile([P, N], F32, name="last%d" % t, tag="last%d" % t) for t in range(TILES)]
                parts = [banks[t][:] for t in range(TILES)]
            for t in range(TILES):
                cols = slice(t * P, (t + 1) * P)
                nc.tensor.matmul_mx(
                    out=parts[t],
                    lhsT=x_codes[:, cols].bitcast(FP8X4),
                    lhsT_scale=x_bytes[:, cols],
                    rhs=w_codes[:].bitcast(FP8X4),
                    rhs_scale=w_bytes[:],
                    start=True,
                    stop=True,
                )
            logits.append(parts)
            if s < SIDES - 1:
                nc.scalar.activation(grown[:, :, s, :], bank[:], ACT.Exp)
            else:
                for t in range(TILES):
                    nc.scalar.activation(grown[:, t, s, :], parts[t], ACT.Exp)

        picked = keep.tile([P, S], F32, name="picked")
        nc.vector.tensor_copy(picked[:], truth_window[:].indirect(offsets[:]))
        capped = keep.tile([P, TILES, SIDES, N], F32, name="capped", tag="wide")
        for t in range(TILES):
            nc.vector.tensor_scalar(capped[:, t], grown[:, t], EXP_CAP, None, ALU.min)
        turned = psum.tile([P, TILES, P], F32, name="turned", tag="spare")
        for t in range(TILES):
            nc.tensor.transpose(turned[:, t, :], picked[:, t * P : (t + 1) * P], identity[:])
        truth = keep.tile([P, TILES, SIDES], F32, name="truth")
        nc.vector.tensor_copy(truth[:], turned[:, :, 0:SIDES])
        extent = keep.tile([P, TILES, 2], F32, name="extent")
        shift = keep.tile([P, TILES, 2], F32, name="shift")
        true_area = keep.tile([P, TILES], F32, name="true_area")
        nc.vector.tensor_tensor(extent[:], truth[:, :, 0:2], truth[:, :, 2:4], ALU.add)
        nc.vector.tensor_tensor(shift[:], truth[:, :, 0:2], truth[:, :, 2:4], ALU.subtract)
        nc.vector.tensor_tensor(true_area[:], extent[:, :, 0], extent[:, :, 1], ALU.mult)

        logs = keep.tile([P, TILES, SIDES, N], F32, name="logs")
        for t in range(TILES):
            step = 1 if t == 0 else 2
            for s in range(0, SIDES, step):
                nc.scalar.activation(logs[:, t, s : s + step, :], capped[:, t, s : s + step, :], ACT.Ln, bias=1.0)

        warm = keep.tile([P, 1], F32, name="warm")
        nc.scalar.activation(warm[:], logs[:, TILES - 1, SIDES - 1, 0:1], ACT.Abs_reciprocal_sqrt)

        def per_tile(name, slots):
            return [keep.tile([P, slots, N], F32, name="%s%d" % (name, t)) for t in range(TILES)]

        dist = per_tile("dist", SIDES)
        near = per_tile("near", 2)
        inner = per_tile("inner", 2)
        size = per_tile("size", 2)
        excess = per_tile("excess", 2)
        skew = per_tile("skew", 2)
        hull_sq = per_tile("hull_sq", 2)
        skew_sq = per_tile("skew_sq", 2)
        areas = per_tile("areas", 2)
        root = per_tile("root", 2)
        half = per_tile("half", 2)
        ratio = per_tile("ratio", 2)
        loss = per_tile("loss", 1)
        union_bank = [psum.tile([P, P], F32, name="union_bank%d" % t) for t in range(TILES)]
        hull_bank = [
            psum.tile([P, P], F32, name="hull_bank%d" % t, tag="spare" if t else "last0") for t in range(TILES)
        ]
        centre_bank = [psum.tile([P, 2, P], F32, name="centre_bank%d" % t, tag="logits%d" % t) for t in range(TILES)]

        def turn_and_add(dest, parts):
            for i, part in enumerate(parts):
                nc.tensor.matmul(
                    dest, lhsT=part, rhs=identity[:], is_transpose=True, start=(i == 0), stop=(i == len(parts) - 1)
                )

        def softplus(t, sides):
            for s in sides:
                nc.vector.tensor_tensor(dist[t][:, s, :], logits[s][t], logs[:, t, s, :], ALU.max)

        def sizes(t):
            for a in range(2):
                nc.vector.tensor_scalar(near[t][:, a, :], dist[t][:, a, :], truth[:, t, a : a + 1], None, ALU.min)
            nc.vector.tensor_tensor(size[t][:], dist[t][:, 0:2, :], dist[t][:, 2:4, :], ALU.add)

        def overlaps(t):
            for a in range(2):
                nc.vector.scalar_tensor_tensor(
                    inner[t][:, a, :], dist[t][:, 2 + a, :], truth[:, t, 2 + a : 3 + a], near[t][:, a, :], ALU.min, ALU.add
                )

        def union(t):
            nc.vector.tensor_tensor(areas[t][:, 0, :], size[t][:, 0, :], size[t][:, 1, :], ALU.mult)
            nc.vector.scalar_tensor_tensor(
                areas[t][:, 1, :], inner[t][:, 0, :], -1.0, inner[t][:, 1, :], ALU.mult, ALU.mult
            )

        def turn_union(t):
            turn_and_add(
                union_bank[t][:],
                [true_area[:, t : t + 1].to_broadcast([P, P]), areas[t][:, 0, :], areas[t][:, 1, :]],
            )

        def turn_overlap(t):
            turn_and_add(centre_bank[t][:, 1, :], [areas[t][:, 1, :]])

        def hull(t):
            nc.vector.tensor_tensor(excess[t][:], size[t][:], inner[t][:], ALU.subtract)
            for a in range(2):
                nc.scalar.activation(hull_sq[t][:, a, :], excess[t][:, a, :], ACT.Square, bias=extent[:, t, a : a + 1])

        def turn_hull(t):
            turn_and_add(hull_bank[t][:], [hull_sq[t][:, a, :] for a in range(2)])

        def centres(t):
            (nc.vector if t else nc.gpsimd).tensor_tensor(skew[t][:], dist[t][:, 2:4, :], dist[t][:, 0:2, :], ALU.subtract)
            for a in range(2):
                nc.scalar.activation(skew_sq[t][:, a, :], skew[t][:, a, :], ACT.Square, bias=shift[:, t, a : a + 1])

        def turn_centres(t):
            turn_and_add(centre_bank[t][:, 0, :], [skew_sq[t][:, a, :] for a in range(2)])

        def reciprocal(t, h, divisor):
            nc.scalar.activation(root[t][:, h, :], divisor, ACT.Abs_reciprocal_sqrt)

        def square_root(t):
            nc.scalar.activation(half[t][:, 1, :], root[t][:, 1, :], ACT.Square)

        def overlap_ratio(t):
            nc.vector.tensor_tensor(half[t][:, 0, :], centre_bank[t][:, 1, :], root[t][:, 0, :], ALU.mult)

        def centre_ratio(t):
            nc.vector.scalar_tensor_tensor(
                ratio[t][:, 1, :], centre_bank[t][:, 0, :], 0.25, half[t][:, 1, :], ALU.mult, ALU.mult
            )

        def second_root(t, h):
            nc.vector.tensor_tensor(ratio[t][:, h, :], half[t][:, h, :], root[t][:, h, :], ALU.mult)

        def finish(t):
            nc.vector.scalar_tensor_tensor(loss[t][:, 0, :], ratio[t][:, 1, :], 1.0, ratio[t][:, 0, :], ALU.add, ALU.add)
            nc.sync.dma_start(out[:, t * P : (t + 1) * P], loss[t][:, 0, :])

        softplus(0, range(SIDES))
        softplus(1, range(SIDES))
        centres(0)
        sizes(0)
        sizes(1)
        overlaps(0)
        overlaps(1)
        hull(0)
        hull(1)
        turn_centres(0)
        turn_hull(0)
        union(0)
        turn_hull(1)
        reciprocal(0, 1, hull_bank[0][:])
        union(1)
        turn_union(0)
        reciprocal(1, 1, hull_bank[1][:])
        centres(1)
        turn_union(1)
        square_root(0)
        reciprocal(0, 0, union_bank[0][:])
        turn_overlap(0)
        turn_overlap(1)
        reciprocal(1, 0, union_bank[1][:])
        square_root(1)
        turn_centres(1)
        centre_ratio(0)
        overlap_ratio(0)
        overlap_ratio(1)
        second_root(0, 0)
        second_root(1, 0)
        centre_ratio(1)
        finish(0)
        finish(1)
